import numpy as np, ml_dtypes
CORES = [83,85,87,115,117,119]
N = 6
import mx_ref
BF = ml_dtypes.bfloat16
def entries(a):
    return np.ascontiguousarray(a.T).reshape(-1)
def table(e):
    return np.ascontiguousarray(np.reshape(e, (-1, 16)).T).astype(np.int32)
def cols(t, e):
    v = np.concatenate([t.reshape(128, -1, 4), np.zeros((128, 1, 4), BF)], axis=1)
    return np.ascontiguousarray(v[:, e]).reshape(128, -1)
def cut(t, i, w=512):
    return t[:, w * i:w * i + w]
def f(rng, *shape):
    return mx_ref.flush((rng.standard_normal(shape, dtype=np.float32) * np.exp2(rng.integers(-2, 3, shape[:-1] + (1,)))).astype(BF))
def wide(rng, *shape, cols=0):
    v = rng.standard_normal(shape, dtype=np.float32) * np.exp2(rng.integers(-12, 13, shape)).astype(np.float32)
    if cols: v *= np.repeat(np.exp2(rng.integers(-cols, cols + 1, shape[:-2] + (1, shape[-1] // 4))) * (rng.random(shape[:-2] + (1, shape[-1] // 4)) > 0.0625), 4, axis=-1).astype(np.float32)
    return mx_ref.flush(v.astype(BF))
C, R, CAPP = 192, 3, 32
def lists(rng, full=False, stay=False, fresh=False, one=False):
    sl = np.full((N, R, N, CAPP), -1); pa = rng.integers(0, C, (N, R, C))
    for t in range(R):
        if stay: continue
        for r in range(N):
            for d in range(N):
                if d == r: continue
                n = CAPP if full else rng.integers(0, CAPP + 1)
                sl[r, t, d, rng.permutation(CAPP)[:n]] = rng.integers(0, C, n)
        for d in range(N):
            far = C + np.flatnonzero(sl[:, t, d].reshape(-1) >= 0)
            pa[d, t, rng.permutation(C)[:far.size]] = far
            if full: continue
            if far.size: pa[d, t, rng.integers(0, C, C // 16)] = rng.choice(far, C // 16)
            pa[d, t, rng.permutation(C)[:C // 2 if fresh else C // 8]] = -1
    if fresh: pa[rng.integers(0, N), rng.integers(0, R)] = -1
    if one:
        o, j = rng.integers(0, N), rng.integers(0, C)
        for t in range(R - 1):
            q, c, k = (o + rng.integers(1, N)) % N, rng.integers(0, CAPP), rng.integers(0, C)
            sl[o, t, q, c] = j; pa[q, t, k] = C + o * CAPP + c
            o, j = q, k
        for q in range(N):
            c = rng.integers(0, CAPP)
            if q != o: sl[o, R - 1, q, c] = j
            pa[q, R - 1] = j if q == o else C + o * CAPP + c
    return {"sl": np.stack([table(sl[r]) for r in range(N)]), "pa": np.stack([table(pa[r]) for r in range(N)])}
def setup_inputs(rng):
    return {"x": f(rng, N, 128, 4 * C * (R + 1)), "w": f(rng, N, 128, 512 * (R + 1)), **lists(rng)}
def setup_inputs_stay(rng):
    return {**setup_inputs(rng), **lists(rng, stay=True)}
def setup_inputs_far(rng):
    return {**setup_inputs(rng), **lists(rng, full=True)}
def setup_inputs_one(rng):
    return {**setup_inputs(rng), **lists(rng, one=True)}
def setup_inputs_fresh(rng):
    return {**setup_inputs(rng), **lists(rng, fresh=True)}
def setup_inputs_spread(rng):
    d = setup_inputs(rng); d["x"] = wide(rng, N, 128, 4 * C * (R + 1), cols=8); return d
def check_inputs(d):
    b = []
    s = [entries(d["sl"][r]).reshape(R, N, CAPP) for r in range(N)]
    for r in range(N):
        p = entries(d["pa"][r]).reshape(R, C)
        if s[r].min() < -1 or s[r].max() >= C or (s[r][:, r] != -1).any(): b.append("sl")
        if p.min() < -1 or p.max() >= C + N * CAPP: b.append("pa"); continue
        for t in range(R):
            slots = np.concatenate([s[q][t, r] for q in range(N)])
            if (slots[p[t][p[t] >= C] - C] < 0).any(): b.append("pa"); break
    return b
def reference(x, w, sl, pa):
    s = [entries(sl[r]).reshape(R, N, CAPP) for r in range(N)]
    p = [entries(pa[r]).reshape(R, C) for r in range(N)]
    cache = [np.ascontiguousarray(cut(x[r], 0, 4 * C)) for r in range(N)]
    y = np.zeros((N, 128, C * (R + 1)), np.float32)
    for t in range(R + 1):
        if t > 0:
            after = []
            for r in range(N):
                slots = [cols(cache[q], s[q][t - 1, r]) for q in range(N)]
                every = np.concatenate([cache[r]] + slots + [cut(x[r], t, 4 * C)], axis=1)
                v = p[r][t - 1]
                after.append(cols(every, np.where(v < 0, C + N * CAPP + np.arange(C), v)))
            cache = after
        for r in range(N):
            y[r][:, C * t:C * t + C] = mx_ref.matmul(mx_ref.quantize(np.ascontiguousarray(cut(w[r], t))), mx_ref.quantize(cache[r]))
    return {"y": y}

@@ -1,0 +1,303 @@
+from concourse.bass import DstId, RemoteDMATransfer
+from concourse.mybir import dt, AluOpType, ActivationFunctionType
+
+C, R, CAPP, N = 192, 3, 32, 6
+WIN = 3 * C
+NEW = 2 * C
+H = C // 16
+Q4 = 128 // 4
+
+CODE, PLANE = "float8_e4m3fn_x4", "uint8"
+SCRATCH = {
+    "xb": ("sbuf", [128, 4 * C * (R + 1)], "bfloat16"),
+    "wb": ("sbuf", [128, 512 * (R + 1)], "bfloat16"),
+    "wq": ("sbuf", [128, 128 * (R + 1)], CODE), "ws": ("sbuf", [128, 128 * (R + 1)], PLANE),
+    "k0q": ("sbuf", [128, C], CODE), "k0s": ("sbuf", [128, C], PLANE),
+    "k3q": ("sbuf", [128, C], CODE), "k3s": ("sbuf", [128, C], PLANE),
+    "yb": ("sbuf", [128, C * (R + 1)], "float32"),
+    "ps": ("psum", [128, 512 * (R + 1)], "float32"),
+    "rsl": ("sbuf", [128, 3 * H], "int32"), "rpa": ("sbuf", [128, 3 * H], "int32"),
+    "row": ("sbuf", [128, 2 * C], "int32"),
+    "prow0": ("sbuf", [128, C], "int32"), "prow1": ("sbuf", [128, C], "int32"),
+    "ioA": ("sbuf", [128, C], "int32"), "ioB": ("sbuf", [128, C], "int32"),
+    "ioJ": ("sbuf", [128, 3 * H], "int32"), "ioK": ("sbuf", [128, 3 * H], "int32"),
+    "dmA": ("sbuf", [128, C], "int32"), "dmask": ("sbuf", [128, C], "float32"), "rmask": ("sbuf", [128, C], "float32"),
+    "jl": ("sbuf", [128, 3 * H], "int32"), "jt": ("sbuf", [128, 3 * H], "int32"),
+    "o1": ("sbuf", [128, H], "uint16"), "o2": ("sbuf", [128, H], "uint16"), "o3": ("sbuf", [128, H], "uint16"),
+    "po": ("sbuf", [128, 3 * H], "uint16"), "ox": ("sbuf", [128, 2 * H], "uint16"),
+    "t384": ("sbuf", [128, 2 * H], "float32"),
+    "xa": ("sbuf", [128, 2 * H], "int32"), "xc": ("sbuf", [128, 2 * H], "int32"),
+    "xh": ("sbuf", [128, 2 * H], "int32"), "xd": ("sbuf", [128, 2 * H], "int32"),
+    "pu": ("sbuf", [128, 3 * H], "int32"), "pm": ("sbuf", [128, 3 * H], "int32"), "pr": ("sbuf", [128, 3 * H], "int32"),
+}
+for _k in range(2):
+    SCRATCH["m%d" % _k] = ("sbuf", [128, C], "float32")
+    SCRATCH["z%d" % _k] = ("sbuf", [128, C], "float32")
+    for _n in ("u", "v", "w"):
+        SCRATCH["c%s%d" % (_n, _k)] = ("sbuf", [128, H], "float32")
+for _t in range(R):
+    SCRATCH["win%dq" % _t] = ("sbuf", [128, WIN], CODE)
+    SCRATCH["win%ds" % _t] = ("sbuf", [128, WIN], PLANE)
+    SCRATCH["sn%dq" % (_t + 1)] = ("sbuf", [128, C], CODE)
+    SCRATCH["sn%ds" % (_t + 1)] = ("sbuf", [128, C], PLANE)
+
+SEMAPHORES = (["lx0", "lx1", "lx2", "lx3", "lw", "lsl", "lpa", "lr0", "lr1", "st", "iot", "bc0", "bc1",
+               "vc", "o1r", "o2r", "o3r", "por", "q0", "nw0", "nw1", "nw2", "qw", "go1", "go2", "left"]
+              + ["%s%d" % (n, t) for t in (1, 2, 3) for n in ("pq", "ps", "kq", "ks", "arq", "ars")]
+              + ["mm%d" % t for t in range(4)] + ["yc%d" % t for t in range(4)])
+
+
+def peers(topo, cores, r):
+    n = len(cores)
+    off, on = [], []
+    for k in range(n):
+        d = (r + n // 2 + k) % n
+        if d != r:
+            (on if topo.chip(cores[d]) == topo.chip(cores[r]) else off).append(d)
+    return off, on
+
+
+def bits(es):
+    return sum(1 << e for e in es)
+
+
+def engines_of(topo, cores, r):
+    off, on = peers(topo, cores, r)
+    far = topo.engines(cores[r], cores[off[0]])
+    near = [e for e in topo.engines(cores[r], cores[on[0]]) if e not in far]
+    h, q = len(far) // 2, len(far) // 4
+    a, b = far[:h], far[h:]
+    plan = {off[0]: (a, b), off[1]: (b[:q], a[:q]), off[2]: (b[q:], a[q:])}
+    k = len(near) // 2
+    for i, d in enumerate(on):
+        plan[d] = (near[i * k:i * k + k], near[i * k:i * k + k])
+    return plan
+
+
+def rank_program(g, core, T, topo):
+    r = T.rank_of(core)
+    if r is None:
+        return
+    S, V, A, Y = T.sem, g.vector, g.scalar, g.sync
+    cores = list(T.cores)
+    plan = engines_of(topo, cores, r)
+    off, on = peers(topo, cores, r)
+    off, on = sorted(off), sorted(on)
+    arrive = [0, 0]
+    for q in range(N):
+        if q != r:
+            e = engines_of(topo, cores, q)[r]
+            arrive[0] += len(e[0])
+            arrive[1] += len(e[1])
+    at = {1: {d: CAPP * d for d in range(N)}}
+    packed = {d: CAPP * i for i, d in enumerate(off + on)}
+    at[2] = at[3] = packed
+    runs = []
+    for d in off + on:
+        if runs and runs[-1][0] + runs[-1][1] == d:
+            runs[-1][1] += 1
+        else:
+            runs.append([d, 1, packed[d] // 16])
+
+    XP = 4 * C
+
+    def load_x(t):
+        Y.dma_start(T.xb[:, XP * t:XP * t + XP], T.x[:, XP * t:XP * t + XP]).then_inc(S["lx%d" % t], 16)
+
+    load_x(0)
+    A.dma_start(T.rsl[0:16, :], T.sl[:, :]).then_inc(S.lsl, 16)
+    Y.dma_start(T.rsl[16:32, :], T.sl[:, :]).then_inc(S.lsl, 16)
+    A.dma_start(T.row[0:1, 0:C], T.pa[:, 0:H]).then_inc(S.lr0, 16)
+    load_x(1)
+    Y.dma_start(T.rpa[0:16, :], T.pa[:, :]).then_inc(S.lpa, 16)
+    Y.dma_start(T.rpa[16:32, :], T.pa[:, :]).then_inc(S.lpa, 16)
+    Y.dma_start(T.row[0:1, C:2 * C], T.pa[:, H:2 * H]).then_inc(S.lr1, 16)
+    Y.wait_ge(S.go1, 1)
+    load_x(2)
+    Y.dma_start(T.wb[:, :], T.w[:, :]).then_inc(S.lw, 16)
+    Y.wait_ge(S.go2, 1)
+    load_x(3)
+
+    g.iota(T.ioA[:, :], [[0, H], [-1, 16]], 16, 1).then_inc(S.iot, 1)
+    g.iota(T.ioB[:, :], [[0, H], [1, 16]], 0, 0).then_inc(S.iot, 1)
+    g.iota(T.ioJ[0:32, :], [[0, 3 * H]], 0, 1).then_inc(S.iot, 1)
+    g.iota(T.ioK[0:32, :], [[0, 3], [16, H]], NEW, 0).then_inc(S.iot, 1)
+
+    def send(t):
+        for part in range(2):
+            src, dst = T["sn%d%s" % (t, "qs"[part])], T["win%d%s" % (t - 1, "qs"[part])]
+            trs = []
+            for d in off + on:
+                rid, pid = topo.addr(cores[d])[:2]
+                a, b = at[t][d], C + CAPP * r
+                sv, dv = src[:, a:a + CAPP], dst[:, b:b + CAPP]
+                if part == 0:
+                    sv, dv = sv.bitcast(dt.uint8), dv.bitcast(dt.uint8)
+                trs.append(RemoteDMATransfer(dst_ids=[DstId(rid=rid, pnc=pid)], dma_engine_mask=bits(plan[d][part]),
+                                             remote_sem=S["ar%s%d" % ("qs"[part], t)], srcs=[sv], dsts=[dv]))
+            g.wait_ge(S["p%s%d" % ("qs"[part], t)], 1)
+            g.remote_dma_fused(trs, local_sem=S.left)
+
+    g.wait_ge(S.lr0, 16)
+    g.partition_broadcast(T.prow0[:, :], T.row[0:1, 0:C], 128).then_inc(S.bc0, 1)
+    send(1)
+    g.sem_inc(S.go1, 1)
+    g.wait_ge(S.lr1, 16)
+    g.partition_broadcast(T.prow1[:, :], T.row[0:1, C:2 * C], 128).then_inc(S.bc1, 1)
+    send(2)
+    g.sem_inc(S.go2, 1)
+    send(3)
+    g.wait_ge(S.left, R * sum(len(e[0]) + len(e[1]) for e in plan.values()))
+
+    n = [0]
+
+    def own(call):
+        call.then_inc(S.vc, 1)
+        n[0] += 1
+
+    def own_wait():
+        V.wait_ge(S.vc, n[0])
+
+    def quads(f):
+        for k in range(4):
+            f(slice(Q4 * k, Q4 * k + Q4))
+
+    def pick_codes(out, win, n_win, offs, k, sem):
+        V.tensor_copy(T[out][:, 0:16 * k].bitcast(dt.uint32),
+                      T[win][:, 0:n_win].bitcast(dt.uint32).indirect(offs)).then_inc(S[sem], 1)
+
+    def pick_scales(out, win, n_win, offs, k, sem):
+        A.activation(T[out][:, 0:16 * k], T[win][:, 0:n_win].indirect(offs), ActivationFunctionType.Copy).then_inc(S[sem], 1)
+
+    def quantise(q, s, a, t, sem):
+        V.quantize_mx(T[q][:, a:a + C], T[s][:, a:a + C], T.xb[:, XP * t:XP * t + XP]).then_inc(S[sem], 1)
+
+    NS = len(off + on) * CAPP // 16
+    first = T.o1[:, 0:H]
+    pas = [T.po[:, H * t:H * t + H] for t in range(R)]
+    second, third = T.o2[:, 0:NS], T.o3[:, 0:NS]
+
+    V.wait_ge(S.iot, 4)
+    own(V.tensor_scalar(T.dmA[:, :], T.ioA[:, :], 15, None, AluOpType.bitwise_and))
+    own(V.tensor_scalar(T.rmask[:, :], T.ioB[:, :], 0, None, AluOpType.is_gt))
+    own(V.tensor_scalar(T.jl[0:32, :], T.ioJ[0:32, :], 15, None, AluOpType.bitwise_and))
+    own_wait()
+    own(V.tensor_scalar(T.dmask[:, :], T.dmA[:, :], 0, None, AluOpType.is_equal))
+    own(V.tensor_tensor(T.jt[0:32, :], T.jl[0:32, :], T.ioK[0:32, :], AluOpType.add))
+
+    V.wait_ge(S.lsl, 32)
+    quads(lambda p: V.tensor_copy(T.o1[p, :], T.rsl[0:32, 0:H]).then_inc(S.o1r, 1))
+    V.wait_ge(S.lx0, 16)
+    quantise("k0q", "k0s", 0, 0, "q0")
+    V.wait_ge(S.o1r, 4)
+    V.wait_ge(S.q0, 1)
+    pick_codes("sn1q", "k0q", C, first, H, "pq1")
+
+    own(V.tensor_scalar(T.xa[0:32, :], T.rsl[0:32, H:3 * H], 0, H, AluOpType.max, AluOpType.mult))
+    own(V.tensor_scalar(T.xh[0:32, :], T.rsl[0:32, H:3 * H], 4, None, AluOpType.arith_shift_right))
+    quantise("win0q", "win0s", 0, 0, "nw0")
+    own_wait()
+    own(V.tensor_scalar(T.xd[0:32, :], T.xh[0:32, :], 1 - 16 * H, None, AluOpType.mult))
+    quads(lambda p: own(V.tensor_scalar(T.t384[p, :], T.rsl[0:32, H:3 * H], 0, NEW, AluOpType.max, AluOpType.add)))
+    own_wait()
+    own(V.tensor_tensor(T.xc[0:32, :], T.xa[0:32, :], T.xd[0:32, :], AluOpType.add))
+    own_wait()
+    quads(lambda p: own(V.tensor_copy(T.ox[p, :], T.xc[0:32, :])))
+    V.wait_ge(S.lx1, 16)
+    quantise("win0q", "win0s", NEW, 1, "nw0")
+
+    def compose(k, out, sem):
+        m, z, u, v, w = T["m%d" % k], T["z%d" % k], T["cu%d" % k], T["cv%d" % k], T["cw%d" % k]
+        ends = z[:, 15:C:16]
+        V.wait_ge(S["bc%d" % k], 1)
+        own_wait()
+        own(V.tensor_tensor(m[:, :], T["prow%d" % k][:, 0:C].indirect(T.ox[:, H * k:H * k + H]), T.dmask[:, :], AluOpType.mult))
+        own_wait()
+        own(V.tensor_tensor_scan(z[:, :], T.rmask[:, :], m[:, :], 0.0, AluOpType.mult, AluOpType.add))
+        own_wait()
+        own(V.tensor_scalar(u[:, :], ends, -1000.0, None, AluOpType.mult))
+        own_wait()
+        own(V.tensor_tensor(v[:, :], u[:, :], T.t384[:, H * k:H * k + H], AluOpType.min))
+        own_wait()
+        own(V.tensor_tensor(w[:, :], v[:, :], ends, AluOpType.max))
+        own_wait()
+        for d, c, a in runs:
+            V.tensor_copy(T[out][:, a:a + 2 * c], w[:, 2 * d:2 * d + 2 * c]).then_inc(S[sem], 1)
+
+    compose(0, "o2", "o2r")
+
+    V.wait_ge(S.nw0, 2)
+    V.wait_ge(S.o2r, len(runs))
+    V.wait_ge(S.arq1, arrive[0])
+    pick_codes("sn2q", "win0q", WIN, second, NS, "pq2")
+    V.wait_ge(S.lpa, 32)
+    own(V.tensor_scalar(T.pu[0:32, :], T.rpa[0:32, :], -1000, None, AluOpType.mult))
+    own_wait()
+    own(V.tensor_tensor(T.pm[0:32, :], T.pu[0:32, :], T.jt[0:32, :], AluOpType.min))
+    own_wait()
+    own(V.tensor_tensor(T.pr[0:32, :], T.pm[0:32, :], T.rpa[0:32, :], AluOpType.max))
+    own_wait()
+    quads(lambda p: V.tensor_copy(T.po[p, :], T.pr[0:32, :]).then_inc(S.por, 1))
+    V.wait_ge(S.por, 4)
+    pick_codes("win1q", "win0q", WIN, pas[0], H, "kq1")
+    V.wait_ge(S.lx2, 16)
+    quantise("win1q", "win1s", NEW, 2, "nw1")
+    compose(1, "o3", "o3r")
+
+    V.wait_ge(S.kq1, 1)
+    V.wait_ge(S.nw1, 1)
+    V.wait_ge(S.o3r, len(runs))
+    V.wait_ge(S.arq2, arrive[0])
+    pick_codes("sn3q", "win1q", WIN, third, NS, "pq3")
+    pick_codes("win2q", "win1q", WIN, pas[1], H, "kq2")
+    V.wait_ge(S.lw, 16)
+    V.quantize_mx(T.wq[:, :], T.ws[:, :], T.wb[:, :]).then_inc(S.qw, 1)
+    V.wait_ge(S.lx3, 16)
+    quantise("win2q", "win2s", NEW, 3, "nw2")
+
+    V.wait_ge(S.kq2, 1)
+    V.wait_ge(S.nw2, 1)
+    V.wait_ge(S.arq3, arrive[0])
+    pick_codes("k3q", "win2q", WIN, pas[2], H, "kq3")
+    V.wait_ge(S.mm3, 1)
+    V.tensor_copy(T.yb[:, 3 * C:4 * C], T.ps[:, 3 * 512:3 * 512 + C]).then_inc(S.yc3, 1)
+
+    A.wait_ge(S.o1r, 4)
+    A.wait_ge(S.q0, 1)
+    pick_scales("sn1s", "k0s", C, first, H, "ps1")
+    A.wait_ge(S.nw0, 2)
+    A.wait_ge(S.o2r, len(runs))
+    A.wait_ge(S.ars1, arrive[1])
+    pick_scales("sn2s", "win0s", WIN, second, NS, "ps2")
+    A.wait_ge(S.por, 4)
+    pick_scales("win1s", "win0s", WIN, pas[0], H, "ks1")
+    A.wait_ge(S.ks1, 1)
+    A.wait_ge(S.nw1, 1)
+    A.wait_ge(S.o3r, len(runs))
+    A.wait_ge(S.ars2, arrive[1])
+    pick_scales("sn3s", "win1s", WIN, third, NS, "ps3")
+    pick_scales("win2s", "win1s", WIN, pas[1], H, "ks2")
+    for t in range(R):
+        A.wait_ge(S["mm%d" % t], 1)
+        A.activation(T.yb[:, C * t:C * t + C], T.ps[:, 512 * t:512 * t + C], ActivationFunctionType.Copy).then_inc(S["yc%d" % t], 1)
+    A.wait_ge(S.ks2, 1)
+    A.wait_ge(S.nw2, 1)
+    A.wait_ge(S.ars3, arrive[1])
+    pick_scales("k3s", "win2s", WIN, pas[2], H, "ks3")
+
+    def product(t, q, s):
+        g.tensor.matmul_mx(T.ps[:, 512 * t:512 * t + C], T.wq[:, 128 * t:128 * t + 128], T.ws[:, 128 * t:128 * t + 128],
+                           T[q][:, 0:C], T[s][:, 0:C], True, True).then_inc(S["mm%d" % t], 1)
+
+    g.tensor.wait_ge(S.qw, 1)
+    g.tensor.wait_ge(S.q0, 1)
+    product(0, "k0q", "k0s")
+    for t in (1, 2, 3):
+        g.tensor.wait_ge(S["kq%d" % t], 1)
+        g.tensor.wait_ge(S["ks%d" % t], 1)
+        product(t, *(("k3q", "k3s") if t == 3 else ("win%dq" % t, "win%ds" % t)))
+
+    for t in range(R + 1):
+        Y.wait_ge(S["yc%d" % t], 1)
+        Y.dma_start(T.y[:, C * t:C * t + C], T.yb[:, C * t:C * t + C]).then_inc(S.st, 16)
+    Y.wait_ge(S.st, 16 * (R + 1))

@@ -6,6 +6,9 @@ WIN = 3 * C
 NEW = 2 * C
 H = C // 16
 Q4 = 128 // 4
+CUT = 128
+CALLS = (("q", "off"), ("s", "off"), ("q", "on"), ("s", "on"))
+PICKS = ("off", "on")
 
 CODE, PLANE = "float8_e4m3fn_x4", "uint8"
 SCRATCH = {
@@ -15,7 +18,7 @@ SCRATCH = {
     "k0q": ("sbuf", [128, C], CODE), "k0s": ("sbuf", [128, C], PLANE),
     "k3q": ("sbuf", [128, C], CODE), "k3s": ("sbuf", [128, C], PLANE),
     "yb": ("sbuf", [128, C * (R + 1)], "float32"),
-    "ps": ("psum", [128, 512 * (R + 1)], "float32"),
+    "ps": ("psum", [128, 512 * (R + 2)], "float32"),
     "rsl": ("sbuf", [128, 3 * H], "int32"), "rpa": ("sbuf", [128, 3 * H], "int32"),
     "row": ("sbuf", [128, 2 * C], "int32"),
     "prow0": ("sbuf", [128, C], "int32"), "prow1": ("sbuf", [128, C], "int32"),
@@ -41,10 +44,11 @@ for _t in range(R):
     SCRATCH["sn%dq" % (_t + 1)] = ("sbuf", [128, C], CODE)
     SCRATCH["sn%ds" % (_t + 1)] = ("sbuf", [128, C], PLANE)
 
-SEMAPHORES = (["lx0", "lx1", "lx2", "lx3", "lw", "lsl", "lpa", "lr0", "lr1", "st", "iot", "bc0", "bc1",
-               "vc", "o1r", "o2r", "o3r", "por", "q0", "nw0", "nw1", "nw2", "qw", "go1", "go2", "left"]
-              + ["%s%d" % (n, t) for t in (1, 2, 3) for n in ("pq", "ps", "kq", "ks", "arq", "ars")]
-              + ["mm%d" % t for t in range(4)] + ["yc%d" % t for t in range(4)])
+SEMAPHORES = (["lx0", "lx1", "lx2", "lx3", "lw", "lsl", "ls2", "lpa", "lr0", "lr1", "st", "iot", "bc0", "bc1",
+               "va", "vb", "o1r", "o2r", "o3r", "por", "q0", "nw0", "nw1", "nw2", "qw", "go1", "go2", "left"]
+              + ["%s%d" % (n, t) for t in (1, 2, 3) for n in ("kq", "ks", "arq", "ars")]
+              + ["p%s%d%s" % (n, t, w) for t in (1, 2, 3) for n in "qs" for w in PICKS]
+              + ["mm%d" % t for t in range(5)] + ["yc%d" % t for t in range(5)] + ["kq4", "ks4"])
 
 
 def peers(topo, cores, r):
@@ -83,6 +87,7 @@ def rank_program(g, core, T, topo):
     plan = engines_of(topo, cores, r)
     off, on = peers(topo, cores, r)
     off, on = sorted(off), sorted(on)
+    to = {"off": off, "on": on}
     arrive = [0, 0]
     for q in range(N):
         if q != r:
@@ -104,14 +109,20 @@ def rank_program(g, core, T, topo):
     def load_x(t):
         Y.dma_start(T.xb[:, XP * t:XP * t + XP], T.x[:, XP * t:XP * t + XP]).then_inc(S["lx%d" % t], 16)
 
+    def group(queue, buf, src, k, sem):
+        queue.dma_start(T[buf][16 * k:16 * k + 16, :], src[:, :]).then_inc(S[sem], 16)
+
     load_x(0)
-    A.dma_start(T.rsl[0:16, :], T.sl[:, :]).then_inc(S.lsl, 16)
-    Y.dma_start(T.rsl[16:32, :], T.sl[:, :]).then_inc(S.lsl, 16)
+    group(A, "rsl", T.sl, 0, "lsl")
+    group(Y, "rsl", T.sl, 1, "lsl")
     A.dma_start(T.row[0:1, 0:C], T.pa[:, 0:H]).then_inc(S.lr0, 16)
+    for k in (2, 3, 4):
+        group(A, "rsl", T.sl, k, "ls2")
+        group(Y, "rsl", T.sl, k + 3, "ls2")
     load_x(1)
-    Y.dma_start(T.rpa[0:16, :], T.pa[:, :]).then_inc(S.lpa, 16)
-    Y.dma_start(T.rpa[16:32, :], T.pa[:, :]).then_inc(S.lpa, 16)
     Y.dma_start(T.row[0:1, C:2 * C], T.pa[:, H:2 * H]).then_inc(S.lr1, 16)
+    for k in range(8):
+        group(Y, "rpa", T.pa, k, "lpa")
     Y.wait_ge(S.go1, 1)
     load_x(2)
     Y.dma_start(T.wb[:, :], T.w[:, :]).then_inc(S.lw, 16)
@@ -120,22 +131,22 @@ def rank_program(g, core, T, topo):
 
     g.iota(T.ioA[:, :], [[0, H], [-1, 16]], 16, 1).then_inc(S.iot, 1)
     g.iota(T.ioB[:, :], [[0, H], [1, 16]], 0, 0).then_inc(S.iot, 1)
-    g.iota(T.ioJ[0:32, :], [[0, 3 * H]], 0, 1).then_inc(S.iot, 1)
-    g.iota(T.ioK[0:32, :], [[0, 3], [16, H]], NEW, 0).then_inc(S.iot, 1)
+    g.iota(T.ioJ[:, :], [[0, 3 * H]], 0, 1).then_inc(S.iot, 1)
+    g.iota(T.ioK[:, :], [[0, 3], [16, H]], NEW, 0).then_inc(S.iot, 1)
 
     def send(t):
-        for part in range(2):
-            src, dst = T["sn%d%s" % (t, "qs"[part])], T["win%d%s" % (t - 1, "qs"[part])]
+        for part, where in CALLS:
+            src, dst, i = T["sn%d%s" % (t, part)], T["win%d%s" % (t - 1, part)], "qs".index(part)
             trs = []
-            for d in off + on:
+            for d in to[where]:
                 rid, pid = topo.addr(cores[d])[:2]
                 a, b = at[t][d], C + CAPP * r
                 sv, dv = src[:, a:a + CAPP], dst[:, b:b + CAPP]
-                if part == 0:
+                if part == "q":
                     sv, dv = sv.bitcast(dt.uint8), dv.bitcast(dt.uint8)
-                trs.append(RemoteDMATransfer(dst_ids=[DstId(rid=rid, pnc=pid)], dma_engine_mask=bits(plan[d][part]),
-                                             remote_sem=S["ar%s%d" % ("qs"[part], t)], srcs=[sv], dsts=[dv]))
-            g.wait_ge(S["p%s%d" % ("qs"[part], t)], 1)
+                trs.append(RemoteDMATransfer(dst_ids=[DstId(rid=rid, pnc=pid)], dma_engine_mask=bits(plan[d][i]),
+                                             remote_sem=S["ar%s%d" % (part, t)], srcs=[sv], dsts=[dv]))
+            g.wait_ge(S["p%s%d%s" % (part, t, where)], 1)
             g.remote_dma_fused(trs, local_sem=S.left)
 
     g.wait_ge(S.lr0, 16)
@@ -149,155 +160,188 @@ def rank_program(g, core, T, topo):
     send(3)
     g.wait_ge(S.left, R * sum(len(e[0]) + len(e[1]) for e in plan.values()))
 
-    n = [0]
+    n = {"va": 0, "vb": 0}
 
-    def own(call):
-        call.then_inc(S.vc, 1)
-        n[0] += 1
+    def step(chain, call):
+        call.then_inc(S[chain], 1)
+        n[chain] += 1
 
-    def own_wait():
-        V.wait_ge(S.vc, n[0])
+    def need(chain):
+        V.wait_ge(S[chain], n[chain])
 
-    def quads(f):
-        for k in range(4):
-            f(slice(Q4 * k, Q4 * k + Q4))
+    def pick(part, out, o, win, n_win, offs, w, sem):
+        if part == "q":
+            V.tensor_copy(T[out + "q"][:, o:o + w].bitcast(dt.uint32),
+                          T[win + "q"][:, 0:n_win].bitcast(dt.uint32).indirect(offs)).then_inc(S[sem], 1)
+        else:
+            A.activation(T[out + "s"][:, o:o + w], T[win + "s"][:, 0:n_win].indirect(offs), ActivationFunctionType.Copy).then_inc(S[sem], 1)
 
-    def pick_codes(out, win, n_win, offs, k, sem):
-        V.tensor_copy(T[out][:, 0:16 * k].bitcast(dt.uint32),
-                      T[win][:, 0:n_win].bitcast(dt.uint32).indirect(offs)).then_inc(S[sem], 1)
+    def pick_sends(part, t):
+        for w in PICKS:
+            a, b = min(at[t][d] for d in to[w]), max(at[t][d] for d in to[w]) + CAPP
+            pick(part, "sn%d" % t, a, "k0" if t == 1 else "win%d" % (t - 2), C if t == 1 else WIN,
+                 T["o%d" % t][:, a // 16:b // 16], b - a, "p%s%d%s" % (part, t, w))
 
-    def pick_scales(out, win, n_win, offs, k, sem):
-        A.activation(T[out][:, 0:16 * k], T[win][:, 0:n_win].indirect(offs), ActivationFunctionType.Copy).then_inc(S[sem], 1)
+    def pick_cache(part, t):
+        if t < R:
+            pick(part, "win%d" % t, 0, "win%d" % (t - 1), WIN, T.po[:, H * (t - 1):H * t], C, "k%s%d" % (part, t))
+        else:
+            for a, b, k in ((0, CUT, 3), (CUT, C, 4)):
+                h = H * (R - 1)
+                pick(part, "k3", a, "win%d" % (t - 1), WIN, T.po[:, h + a // 16:h + b // 16], b - a, "k%s%d" % (part, k))
 
-    def quantise(q, s, a, t, sem):
-        V.quantize_mx(T[q][:, a:a + C], T[s][:, a:a + C], T.xb[:, XP * t:XP * t + XP]).then_inc(S[sem], 1)
-
-    NS = len(off + on) * CAPP // 16
-    first = T.o1[:, 0:H]
-    pas = [T.po[:, H * t:H * t + H] for t in range(R)]
-    second, third = T.o2[:, 0:NS], T.o3[:, 0:NS]
+    def quantise(b, a, t, sem):
+        V.quantize_mx(T[b + "q"][:, a:a + C], T[b + "s"][:, a:a + C], T.xb[:, XP * t:XP * t + XP]).then_inc(S[sem], 1)
 
     V.wait_ge(S.iot, 4)
-    own(V.tensor_scalar(T.dmA[:, :], T.ioA[:, :], 15, None, AluOpType.bitwise_and))
-    own(V.tensor_scalar(T.rmask[:, :], T.ioB[:, :], 0, None, AluOpType.is_gt))
-    own(V.tensor_scalar(T.jl[0:32, :], T.ioJ[0:32, :], 15, None, AluOpType.bitwise_and))
-    own_wait()
-    own(V.tensor_scalar(T.dmask[:, :], T.dmA[:, :], 0, None, AluOpType.is_equal))
-    own(V.tensor_tensor(T.jt[0:32, :], T.jl[0:32, :], T.ioK[0:32, :], AluOpType.add))
+    step("va", V.tensor_scalar(T.dmA[:, :], T.ioA[:, :], 15, None, AluOpType.bitwise_and))
+    step("vb", V.tensor_scalar(T.jl[:, :], T.ioJ[:, :], 15, None, AluOpType.bitwise_and))
+    need("va")
+    step("va", V.tensor_scalar(T.dmask[:, :], T.dmA[:, :], 0, None, AluOpType.is_equal))
+    need("vb")
+    step("vb", V.tensor_tensor(T.jt[:, :], T.jl[:, :], T.ioK[:, :], AluOpType.add))
+    step("va", V.tensor_scalar(T.rmask[:, :], T.ioB[:, :], 0, None, AluOpType.is_gt))
 
     V.wait_ge(S.lsl, 32)
-    quads(lambda p: V.tensor_copy(T.o1[p, :], T.rsl[0:32, 0:H]).then_inc(S.o1r, 1))
+    for k in range(4):
+        V.tensor_copy(T.o1[Q4 * k:Q4 * k + Q4, :], T.rsl[0:32, 0:H]).then_inc(S.o1r, 1)
     V.wait_ge(S.lx0, 16)
-    quantise("k0q", "k0s", 0, 0, "q0")
+    quantise("k0", 0, 0, "q0")
     V.wait_ge(S.o1r, 4)
     V.wait_ge(S.q0, 1)
-    pick_codes("sn1q", "k0q", C, first, H, "pq1")
+    pick_sends("q", 1)
 
-    own(V.tensor_scalar(T.xa[0:32, :], T.rsl[0:32, H:3 * H], 0, H, AluOpType.max, AluOpType.mult))
-    own(V.tensor_scalar(T.xh[0:32, :], T.rsl[0:32, H:3 * H], 4, None, AluOpType.arith_shift_right))
-    quantise("win0q", "win0s", 0, 0, "nw0")
-    own_wait()
-    own(V.tensor_scalar(T.xd[0:32, :], T.xh[0:32, :], 1 - 16 * H, None, AluOpType.mult))
-    quads(lambda p: own(V.tensor_scalar(T.t384[p, :], T.rsl[0:32, H:3 * H], 0, NEW, AluOpType.max, AluOpType.add)))
-    own_wait()
-    own(V.tensor_tensor(T.xc[0:32, :], T.xa[0:32, :], T.xd[0:32, :], AluOpType.add))
-    own_wait()
-    quads(lambda p: own(V.tensor_copy(T.ox[p, :], T.xc[0:32, :])))
-    V.wait_ge(S.lx1, 16)
-    quantise("win0q", "win0s", NEW, 1, "nw0")
-
-    def compose(k, out, sem):
-        m, z, u, v, w = T["m%d" % k], T["z%d" % k], T["cu%d" % k], T["cv%d" % k], T["cw%d" % k]
-        ends = z[:, 15:C:16]
+    def gather(k):
         V.wait_ge(S["bc%d" % k], 1)
-        own_wait()
-        own(V.tensor_tensor(m[:, :], T["prow%d" % k][:, 0:C].indirect(T.ox[:, H * k:H * k + H]), T.dmask[:, :], AluOpType.mult))
-        own_wait()
-        own(V.tensor_tensor_scan(z[:, :], T.rmask[:, :], m[:, :], 0.0, AluOpType.mult, AluOpType.add))
-        own_wait()
-        own(V.tensor_scalar(u[:, :], ends, -1000.0, None, AluOpType.mult))
-        own_wait()
-        own(V.tensor_tensor(v[:, :], u[:, :], T.t384[:, H * k:H * k + H], AluOpType.min))
-        own_wait()
-        own(V.tensor_tensor(w[:, :], v[:, :], ends, AluOpType.max))
-        own_wait()
-        for d, c, a in runs:
-            V.tensor_copy(T[out][:, a:a + 2 * c], w[:, 2 * d:2 * d + 2 * c]).then_inc(S[sem], 1)
+        need("va")
+        step("va", V.tensor_tensor(T["m%d" % k][:, :], T["prow%d" % k][:, 0:C].indirect(T.ox[:, H * k:H * k + H]),
+                                   T.dmask[:, :], AluOpType.mult))
 
-    compose(0, "o2", "o2r")
+    def scan(k):
+        need("va")
+        step("va", V.tensor_tensor_scan(T["z%d" % k][:, :], T.rmask[:, :], T["m%d" % k][:, :], 0.0, AluOpType.mult, AluOpType.add))
+
+    def ends(k):
+        return T["z%d" % k][:, 15:C:16]
+
+    def fresh1(k):
+        need("va")
+        step("va", V.tensor_scalar(T["cu%d" % k][:, :], ends(k), -1000.0, None, AluOpType.mult))
+
+    def fresh2(k):
+        need("va")
+        step("va", V.tensor_tensor(T["cv%d" % k][:, :], T["cu%d" % k][:, :], T.t384[:, H * k:H * k + H], AluOpType.min))
+
+    def fresh3(k):
+        need("va")
+        step("va", V.tensor_tensor(T["cw%d" % k][:, :], T["cv%d" % k][:, :], ends(k), AluOpType.max))
+
+    def offsets(k, out):
+        need("va")
+        for d, c, a in runs:
+            V.tensor_copy(T[out][:, a:a + 2 * c], T["cw%d" % k][:, 2 * d:2 * d + 2 * c]).then_inc(S[out + "r"], 1)
+
+    V.wait_ge(S.ls2, 96)
+    step("va", V.tensor_scalar(T.xh[:, :], T.rsl[:, H:3 * H], 4, None, AluOpType.arith_shift_right))
+    step("va", V.tensor_scalar(T.xa[:, :], T.rsl[:, H:3 * H], 0, H, AluOpType.max, AluOpType.mult))
+    quantise("win0", 0, 0, "nw0")
+    need("va")
+    step("va", V.tensor_scalar(T.xd[:, :], T.xh[:, :], 1 - 16 * H, None, AluOpType.mult))
+    step("vb", V.tensor_scalar(T.t384[:, :], T.rsl[:, H:3 * H], 0, NEW, AluOpType.max, AluOpType.add))
+    need("va")
+    step("va", V.tensor_tensor(T.xc[:, :], T.xa[:, :], T.xd[:, :], AluOpType.add))
+    need("va")
+    step("va", V.tensor_copy(T.ox[:, :], T.xc[:, :]))
+    gather(0)
+    V.wait_ge(S.lx1, 16)
+    quantise("win0", NEW, 1, "nw0")
+    scan(0)
+    need("vb")
+    fresh1(0)
+    fresh2(0)
+    fresh3(0)
+    offsets(0, "o2")
 
     V.wait_ge(S.nw0, 2)
     V.wait_ge(S.o2r, len(runs))
     V.wait_ge(S.arq1, arrive[0])
-    pick_codes("sn2q", "win0q", WIN, second, NS, "pq2")
-    V.wait_ge(S.lpa, 32)
-    own(V.tensor_scalar(T.pu[0:32, :], T.rpa[0:32, :], -1000, None, AluOpType.mult))
-    own_wait()
-    own(V.tensor_tensor(T.pm[0:32, :], T.pu[0:32, :], T.jt[0:32, :], AluOpType.min))
-    own_wait()
-    own(V.tensor_tensor(T.pr[0:32, :], T.pm[0:32, :], T.rpa[0:32, :], AluOpType.max))
-    own_wait()
-    quads(lambda p: V.tensor_copy(T.po[p, :], T.pr[0:32, :]).then_inc(S.por, 1))
-    V.wait_ge(S.por, 4)
-    pick_codes("win1q", "win0q", WIN, pas[0], H, "kq1")
+    pick_sends("q", 2)
+    V.wait_ge(S.lpa, 128)
+    step("vb", V.tensor_scalar(T.pu[:, :], T.rpa[:, :], -1000, None, AluOpType.mult))
+    gather(1)
+    need("vb")
+    step("vb", V.tensor_tensor(T.pm[:, :], T.pu[:, :], T.jt[:, :], AluOpType.min))
+    scan(1)
+    need("vb")
+    step("vb", V.tensor_tensor(T.pr[:, :], T.pm[:, :], T.rpa[:, :], AluOpType.max))
+    fresh1(1)
+    need("vb")
+    V.tensor_copy(T.po[:, :], T.pr[:, :]).then_inc(S.por, 1)
+    fresh2(1)
+    V.wait_ge(S.por, 1)
+    pick_cache("q", 1)
+    fresh3(1)
     V.wait_ge(S.lx2, 16)
-    quantise("win1q", "win1s", NEW, 2, "nw1")
-    compose(1, "o3", "o3r")
+    quantise("win1", NEW, 2, "nw1")
+    offsets(1, "o3")
 
     V.wait_ge(S.kq1, 1)
     V.wait_ge(S.nw1, 1)
     V.wait_ge(S.o3r, len(runs))
     V.wait_ge(S.arq2, arrive[0])
-    pick_codes("sn3q", "win1q", WIN, third, NS, "pq3")
-    pick_codes("win2q", "win1q", WIN, pas[1], H, "kq2")
+    pick_sends("q", 3)
+    pick_cache("q", 2)
     V.wait_ge(S.lw, 16)
     V.quantize_mx(T.wq[:, :], T.ws[:, :], T.wb[:, :]).then_inc(S.qw, 1)
     V.wait_ge(S.lx3, 16)
-    quantise("win2q", "win2s", NEW, 3, "nw2")
+    quantise("win2", NEW, 3, "nw2")
 
     V.wait_ge(S.kq2, 1)
     V.wait_ge(S.nw2, 1)
     V.wait_ge(S.arq3, arrive[0])
-    pick_codes("k3q", "win2q", WIN, pas[2], H, "kq3")
-    V.wait_ge(S.mm3, 1)
-    V.tensor_copy(T.yb[:, 3 * C:4 * C], T.ps[:, 3 * 512:3 * 512 + C]).then_inc(S.yc3, 1)
+    pick_cache("q", 3)
+    V.wait_ge(S.mm4, 1)
+    V.tensor_copy(T.yb[:, 3 * C + CUT:4 * C], T.ps[:, 4 * 512 + 2 * CUT - C:4 * 512 + CUT]).then_inc(S.yc4, 1)
 
     A.wait_ge(S.o1r, 4)
     A.wait_ge(S.q0, 1)
-    pick_scales("sn1s", "k0s", C, first, H, "ps1")
+    pick_sends("s", 1)
     A.wait_ge(S.nw0, 2)
     A.wait_ge(S.o2r, len(runs))
     A.wait_ge(S.ars1, arrive[1])
-    pick_scales("sn2s", "win0s", WIN, second, NS, "ps2")
-    A.wait_ge(S.por, 4)
-    pick_scales("win1s", "win0s", WIN, pas[0], H, "ks1")
+    pick_sends("s", 2)
+    A.wait_ge(S.por, 1)
+    pick_cache("s", 1)
     A.wait_ge(S.ks1, 1)
     A.wait_ge(S.nw1, 1)
     A.wait_ge(S.o3r, len(runs))
     A.wait_ge(S.ars2, arrive[1])
-    pick_scales("sn3s", "win1s", WIN, third, NS, "ps3")
-    pick_scales("win2s", "win1s", WIN, pas[1], H, "ks2")
+    pick_sends("s", 3)
+    pick_cache("s", 2)
     for t in range(R):
         A.wait_ge(S["mm%d" % t], 1)
         A.activation(T.yb[:, C * t:C * t + C], T.ps[:, 512 * t:512 * t + C], ActivationFunctionType.Copy).then_inc(S["yc%d" % t], 1)
     A.wait_ge(S.ks2, 1)
     A.wait_ge(S.nw2, 1)
     A.wait_ge(S.ars3, arrive[1])
-    pick_scales("k3s", "win2s", WIN, pas[2], H, "ks3")
+    pick_cache("s", 3)
+    A.wait_ge(S.mm3, 1)
+    A.activation(T.yb[:, 3 * C:3 * C + CUT], T.ps[:, 3 * 512:3 * 512 + CUT], ActivationFunctionType.Copy).then_inc(S.yc3, 1)
 
-    def product(t, q, s):
-        g.tensor.matmul_mx(T.ps[:, 512 * t:512 * t + C], T.wq[:, 128 * t:128 * t + 128], T.ws[:, 128 * t:128 * t + 128],
-                           T[q][:, 0:C], T[s][:, 0:C], True, True).then_inc(S["mm%d" % t], 1)
+    def product(k, b, a, w):
+        t = min(k, R)
+        g.tensor.matmul_mx(T.ps[:, 512 * k:512 * k + w], T.wq[:, 128 * t:128 * t + 128], T.ws[:, 128 * t:128 * t + 128],
+                           T[b + "q"][:, a:a + w], T[b + "s"][:, a:a + w], True, True).then_inc(S["mm%d" % k], 1)
 
     g.tensor.wait_ge(S.qw, 1)
     g.tensor.wait_ge(S.q0, 1)
-    product(0, "k0q", "k0s")
-    for t in (1, 2, 3):
-        g.tensor.wait_ge(S["kq%d" % t], 1)
-        g.tensor.wait_ge(S["ks%d" % t], 1)
-        product(t, *(("k3q", "k3s") if t == 3 else ("win%dq" % t, "win%ds" % t)))
+    product(0, "k0", 0, C)
+    for k, b, a, w in ((1, "win1", 0, C), (2, "win2", 0, C), (3, "k3", 0, CUT), (4, "k3", C - CUT, CUT)):
+        g.tensor.wait_ge(S["kq%d" % k], 1)
+        g.tensor.wait_ge(S["ks%d" % k], 1)
+        product(k, b, a, w)
 
-    for t in range(R + 1):
-        Y.wait_ge(S["yc%d" % t], 1)
-        Y.dma_start(T.y[:, C * t:C * t + C], T.yb[:, C * t:C * t + C]).then_inc(S.st, 16)
-    Y.wait_ge(S.st, 16 * (R + 1))
+    for k, (a, b) in enumerate(((0, C), (C, 2 * C), (2 * C, 3 * C), (3 * C, 3 * C + CUT), (3 * C + CUT, 4 * C))):
+        Y.wait_ge(S["yc%d" % k], 1)
+        Y.dma_start(T.y[:, a:b], T.yb[:, a:b]).then_inc(S.st, 16)
+    Y.wait_ge(S.st, 16 * (R + 2))

@@ -6,9 +6,11 @@ WIN = 3 * C
 NEW = 2 * C
 H = C // 16
 Q4 = 128 // 4
-CUT = 128
-CALLS = (("q", "off"), ("s", "off"), ("q", "on"), ("s", "on"))
-PICKS = ("off", "on")
+MIN = 128
+BANK = 512
+PARTS = ("a", "b")
+CALLS = {1: (("q", "a"), ("s", "a"), ("q", "b"), ("s", "b"))}
+CALLS[2] = CALLS[3] = (("q", "a"), ("q", "b"), ("s", "a"), ("s", "b"))
 
 CODE, PLANE = "float8_e4m3fn_x4", "uint8"
 SCRATCH = {
@@ -16,27 +18,23 @@ SCRATCH = {
     "wb": ("sbuf", [128, 512 * (R + 1)], "bfloat16"),
     "wq": ("sbuf", [128, 128 * (R + 1)], CODE), "ws": ("sbuf", [128, 128 * (R + 1)], PLANE),
     "k0q": ("sbuf", [128, C], CODE), "k0s": ("sbuf", [128, C], PLANE),
-    "k3q": ("sbuf", [128, C], CODE), "k3s": ("sbuf", [128, C], PLANE),
-    "yb": ("sbuf", [128, C * (R + 1)], "float32"),
-    "ps": ("psum", [128, 512 * (R + 2)], "float32"),
+    "yb": ("sbuf", [128, C * (R + 1)], "float32"), "yw": ("sbuf", [128, WIN], "float32"),
+    "ps": ("psum", [128, BANK * 7], "float32"),
     "rsl": ("sbuf", [128, 3 * H], "int32"), "rpa": ("sbuf", [128, 3 * H], "int32"),
-    "row": ("sbuf", [128, 2 * C], "int32"),
-    "prow0": ("sbuf", [128, C], "int32"), "prow1": ("sbuf", [128, C], "int32"),
-    "ioA": ("sbuf", [128, C], "int32"), "ioB": ("sbuf", [128, C], "int32"),
+    "rsh": ("sbuf", [128, 2 * H], "int32"), "row": ("sbuf", [128, 2 * C], "int32"),
+    "xh": ("sbuf", [128, H], "int32"), "xa": ("sbuf", [128, H], "int32"),
+    "xd": ("sbuf", [128, H], "int32"), "xc": ("sbuf", [128, H], "int32"), "ox": ("sbuf", [128, 2 * H], "uint16"),
+    "tp": ("sbuf", [128, 2 * H], "float32"), "tn": ("sbuf", [128, 2 * H], "float32"),
     "ioJ": ("sbuf", [128, 3 * H], "int32"), "ioK": ("sbuf", [128, 3 * H], "int32"),
-    "dmA": ("sbuf", [128, C], "int32"), "dmask": ("sbuf", [128, C], "float32"), "rmask": ("sbuf", [128, C], "float32"),
     "jl": ("sbuf", [128, 3 * H], "int32"), "jt": ("sbuf", [128, 3 * H], "int32"),
+    "pu": ("sbuf", [128, 3 * H], "int32"), "pr": ("sbuf", [128, 3 * H], "int32"),
     "o1": ("sbuf", [128, H], "uint16"), "o2": ("sbuf", [128, H], "uint16"), "o3": ("sbuf", [128, H], "uint16"),
-    "po": ("sbuf", [128, 3 * H], "uint16"), "ox": ("sbuf", [128, 2 * H], "uint16"),
-    "t384": ("sbuf", [128, 2 * H], "float32"),
-    "xa": ("sbuf", [128, 2 * H], "int32"), "xc": ("sbuf", [128, 2 * H], "int32"),
-    "xh": ("sbuf", [128, 2 * H], "int32"), "xd": ("sbuf", [128, 2 * H], "int32"),
-    "pu": ("sbuf", [128, 3 * H], "int32"), "pm": ("sbuf", [128, 3 * H], "int32"), "pr": ("sbuf", [128, 3 * H], "int32"),
+    "po": ("sbuf", [128, 3 * H], "uint16"),
 }
 for _k in range(2):
     SCRATCH["m%d" % _k] = ("sbuf", [128, C], "float32")
     SCRATCH["z%d" % _k] = ("sbuf", [128, C], "float32")
-    for _n in ("u", "v", "w"):
+    for _n in ("u", "w"):
         SCRATCH["c%s%d" % (_n, _k)] = ("sbuf", [128, H], "float32")
 for _t in range(R):
     SCRATCH["win%dq" % _t] = ("sbuf", [128, WIN], CODE)
@@ -44,34 +42,39 @@ for _t in range(R):
     SCRATCH["sn%dq" % (_t + 1)] = ("sbuf", [128, C], CODE)
     SCRATCH["sn%ds" % (_t + 1)] = ("sbuf", [128, C], PLANE)
 
-SEMAPHORES = (["lx0", "lx1", "lx2", "lx3", "lw", "lsl", "ls2", "lpa", "lr0", "lr1", "st", "iot", "bc0", "bc1",
-               "va", "vb", "o1r", "o2r", "o3r", "por", "q0", "nw0", "nw1", "nw2", "qw", "go1", "go2", "left"]
+SEMAPHORES = (["lx0", "lx1", "lx2", "lx3", "lw0", "lw2", "lsl", "ls2", "lsh", "lpa", "lrow", "st", "mz", "iot",
+               "va", "vb", "o1r", "o2r", "o3r", "por", "q0", "nw0", "nw1", "nw2", "qw0", "qw2", "lq1", "lq2", "left",
+               "kfq", "kfs", "anq", "ans", "ywr"]
               + ["%s%d" % (n, t) for t in (1, 2, 3) for n in ("kq", "ks", "arq", "ars")]
-              + ["p%s%d%s" % (n, t, w) for t in (1, 2, 3) for n in "qs" for w in PICKS]
-              + ["mm%d" % t for t in range(5)] + ["yc%d" % t for t in range(5)] + ["kq4", "ks4"])
+              + ["p%s%d%s" % (n, t, w) for t in (1, 2, 3) for n in "qs" for w in PARTS]
+              + ["mm%d" % t for t in range(7)] + ["yc%d" % t for t in range(4)])
 
 
 def peers(topo, cores, r):
-    n = len(cores)
-    off, on = [], []
-    for k in range(n):
-        d = (r + n // 2 + k) % n
-        if d != r:
-            (on if topo.chip(cores[d]) == topo.chip(cores[r]) else off).append(d)
-    return off, on
+    ds = [d for d in range(len(cores)) if d != r]
+    home = topo.chip(cores[r])
+    return [d for d in ds if topo.chip(cores[d]) != home], [d for d in ds if topo.chip(cores[d]) == home]
 
 
 def bits(es):
     return sum(1 << e for e in es)
 
 
-def engines_of(topo, cores, r):
+def parts_of(topo, cores, r, t):
+    off, on = peers(topo, cores, r)
+    return {"a": off, "b": on} if t == 1 else {"a": off[:2], "b": off[2:] + on}
+
+
+def engines_of(topo, cores, r, t):
     off, on = peers(topo, cores, r)
     far = topo.engines(cores[r], cores[off[0]])
     near = [e for e in topo.engines(cores[r], cores[on[0]]) if e not in far]
     h, q = len(far) // 2, len(far) // 4
     a, b = far[:h], far[h:]
-    plan = {off[0]: (a, b), off[1]: (b[:q], a[:q]), off[2]: (b[q:], a[q:])}
+    if t == 1:
+        plan = {off[0]: (a, b), off[1]: (b[:q], a[:q]), off[2]: (b[q:], a[q:])}
+    else:
+        plan = {off[0]: (a, a), off[1]: (b, b), off[2]: (far, far)}
     k = len(near) // 2
     for i, d in enumerate(on):
         plan[d] = (near[i * k:i * k + k], near[i * k:i * k + k])
@@ -84,81 +87,82 @@ def rank_program(g, core, T, topo):
         return
     S, V, A, Y = T.sem, g.vector, g.scalar, g.sync
     cores = list(T.cores)
-    plan = engines_of(topo, cores, r)
+    rounds = range(1, R + 1)
     off, on = peers(topo, cores, r)
-    off, on = sorted(off), sorted(on)
-    to = {"off": off, "on": on}
-    arrive = [0, 0]
-    for q in range(N):
-        if q != r:
-            e = engines_of(topo, cores, q)[r]
-            arrive[0] += len(e[0])
-            arrive[1] += len(e[1])
+    plan = {t: engines_of(topo, cores, r, t) for t in rounds}
+    to = {t: parts_of(topo, cores, r, t) for t in rounds}
+
+    def arrive(t, part, sources):
+        return sum(len(engines_of(topo, cores, q, t)[r]["qs".index(part)]) for q in sources)
+
+    order = to[2]["a"] + to[2]["b"]
     at = {1: {d: CAPP * d for d in range(N)}}
-    packed = {d: CAPP * i for i, d in enumerate(off + on)}
-    at[2] = at[3] = packed
+    at[2] = at[3] = {d: CAPP * i for i, d in enumerate(order)}
     runs = []
-    for d in off + on:
+    for d in order:
         if runs and runs[-1][0] + runs[-1][1] == d:
             runs[-1][1] += 1
         else:
-            runs.append([d, 1, packed[d] // 16])
+            runs.append([d, 1, at[2][d] // 16])
 
     XP = 4 * C
 
     def load_x(t):
         Y.dma_start(T.xb[:, XP * t:XP * t + XP], T.x[:, XP * t:XP * t + XP]).then_inc(S["lx%d" % t], 16)
 
+    def load_w(a, b):
+        Y.dma_start(T.wb[:, 512 * a:512 * b], T.w[:, 512 * a:512 * b]).then_inc(S["lw%d" % a], 16)
+
     def group(queue, buf, src, k, sem):
         queue.dma_start(T[buf][16 * k:16 * k + 16, :], src[:, :]).then_inc(S[sem], 16)
 
+    def behind(t):
+        Y.wait_ge(S["lq%d" % t], sum(len(plan[t][d][0]) for d in to[t]["a"]))
+
     load_x(0)
     group(A, "rsl", T.sl, 0, "lsl")
-    group(Y, "rsl", T.sl, 1, "lsl")
-    A.dma_start(T.row[0:1, 0:C], T.pa[:, 0:H]).then_inc(S.lr0, 16)
-    for k in (2, 3, 4):
-        group(A, "rsl", T.sl, k, "ls2")
-        group(Y, "rsl", T.sl, k + 3, "ls2")
+    group(A, "rsl", T.sl, 1, "lsl")
+    for k in range(8):
+        o = k % 2
+        A.dma_start(T.rsh[16 * k:16 * k + 16, 0:2 * H - o], T.sl[:, H + o:3 * H]).then_inc(S.lsh, 16)
+    Y.wait_ge(S.mz, 1)
+    for k in range(8):
+        Y.dma_start(T.row[16 * k:16 * k + 1, :], T.pa[:, 0:2 * H]).then_inc(S.lrow, 16)
+    for k in range(2, 8):
+        group(Y, "rsl", T.sl, k, "ls2")
     load_x(1)
-    Y.dma_start(T.row[0:1, C:2 * C], T.pa[:, H:2 * H]).then_inc(S.lr1, 16)
+    load_w(0, 2)
     for k in range(8):
         group(Y, "rpa", T.pa, k, "lpa")
-    Y.wait_ge(S.go1, 1)
     load_x(2)
-    Y.dma_start(T.wb[:, :], T.w[:, :]).then_inc(S.lw, 16)
-    Y.wait_ge(S.go2, 1)
+    behind(1)
+    load_w(2, 4)
+    behind(2)
     load_x(3)
 
-    g.iota(T.ioA[:, :], [[0, H], [-1, 16]], 16, 1).then_inc(S.iot, 1)
-    g.iota(T.ioB[:, :], [[0, H], [1, 16]], 0, 0).then_inc(S.iot, 1)
     g.iota(T.ioJ[:, :], [[0, 3 * H]], 0, 1).then_inc(S.iot, 1)
-    g.iota(T.ioK[:, :], [[0, 3], [16, H]], NEW, 0).then_inc(S.iot, 1)
+    g.iota(T.ioK[:, :], [[0, R], [-16, H]], -NEW, 0).then_inc(S.iot, 1)
 
-    def send(t):
-        for part, where in CALLS:
+    waits = 0
+    for t in rounds:
+        for part, where in CALLS[t]:
             src, dst, i = T["sn%d%s" % (t, part)], T["win%d%s" % (t - 1, part)], "qs".index(part)
-            trs = []
-            for d in to[where]:
+            trs, n = [], 0
+            for d in to[t][where]:
                 rid, pid = topo.addr(cores[d])[:2]
                 a, b = at[t][d], C + CAPP * r
                 sv, dv = src[:, a:a + CAPP], dst[:, b:b + CAPP]
                 if part == "q":
                     sv, dv = sv.bitcast(dt.uint8), dv.bitcast(dt.uint8)
-                trs.append(RemoteDMATransfer(dst_ids=[DstId(rid=rid, pnc=pid)], dma_engine_mask=bits(plan[d][i]),
-                                             remote_sem=S["ar%s%d" % (part, t)], srcs=[sv], dsts=[dv]))
+                sem = "an" + part if t == R and d in on else "ar%s%d" % (part, t)
+                trs.append(RemoteDMATransfer(dst_ids=[DstId(rid=rid, pnc=pid)], dma_engine_mask=bits(plan[t][d][i]),
+                                             remote_sem=S[sem], srcs=[sv], dsts=[dv]))
+                n += len(plan[t][d][i])
+            first = t < R and (part, where) == CALLS[t][0]
+            waits += 0 if first else n
             g.wait_ge(S["p%s%d%s" % (part, t, where)], 1)
-            g.remote_dma_fused(trs, local_sem=S.left)
-
-    g.wait_ge(S.lr0, 16)
-    g.partition_broadcast(T.prow0[:, :], T.row[0:1, 0:C], 128).then_inc(S.bc0, 1)
-    send(1)
-    g.sem_inc(S.go1, 1)
-    g.wait_ge(S.lr1, 16)
-    g.partition_broadcast(T.prow1[:, :], T.row[0:1, C:2 * C], 128).then_inc(S.bc1, 1)
-    send(2)
-    g.sem_inc(S.go2, 1)
-    send(3)
-    g.wait_ge(S.left, R * sum(len(e[0]) + len(e[1]) for e in plan.values()))
+            g.remote_dma_fused(trs, local_sem=S["lq%d" % t] if first else S.left)
+    g.wait_ge(S.left, waits)
 
     n = {"va": 0, "vb": 0}
 
@@ -177,31 +181,26 @@ def rank_program(g, core, T, topo):
             A.activation(T[out + "s"][:, o:o + w], T[win + "s"][:, 0:n_win].indirect(offs), ActivationFunctionType.Copy).then_inc(S[sem], 1)
 
     def pick_sends(part, t):
-        for w in PICKS:
-            a, b = min(at[t][d] for d in to[w]), max(at[t][d] for d in to[w]) + CAPP
+        for w in PARTS:
+            a, b = min(at[t][d] for d in to[t][w]), max(at[t][d] for d in to[t][w]) + CAPP
             pick(part, "sn%d" % t, a, "k0" if t == 1 else "win%d" % (t - 2), C if t == 1 else WIN,
                  T["o%d" % t][:, a // 16:b // 16], b - a, "p%s%d%s" % (part, t, w))
 
     def pick_cache(part, t):
-        if t < R:
-            pick(part, "win%d" % t, 0, "win%d" % (t - 1), WIN, T.po[:, H * (t - 1):H * t], C, "k%s%d" % (part, t))
-        else:
-            for a, b, k in ((0, CUT, 3), (CUT, C, 4)):
-                h = H * (R - 1)
-                pick(part, "k3", a, "win%d" % (t - 1), WIN, T.po[:, h + a // 16:h + b // 16], b - a, "k%s%d" % (part, k))
+        pick(part, "win%d" % t, 0, "win%d" % (t - 1), WIN, T.po[:, H * (t - 1):H * t], C, "k%s%d" % (part, t))
+
+    def fill_own(part):
+        t = R - 1
+        pick(part, "win%d" % t, C + CAPP * r, "win%d" % (t - 1), WIN, T.po[:, H * (t - 1):H * (t - 1) + CAPP // 16], CAPP, "kf" + part)
 
     def quantise(b, a, t, sem):
         V.quantize_mx(T[b + "q"][:, a:a + C], T[b + "s"][:, a:a + C], T.xb[:, XP * t:XP * t + XP]).then_inc(S[sem], 1)
 
-    V.wait_ge(S.iot, 4)
-    step("va", V.tensor_scalar(T.dmA[:, :], T.ioA[:, :], 15, None, AluOpType.bitwise_and))
-    step("vb", V.tensor_scalar(T.jl[:, :], T.ioJ[:, :], 15, None, AluOpType.bitwise_and))
-    need("va")
-    step("va", V.tensor_scalar(T.dmask[:, :], T.dmA[:, :], 0, None, AluOpType.is_equal))
-    need("vb")
-    step("vb", V.tensor_tensor(T.jt[:, :], T.jl[:, :], T.ioK[:, :], AluOpType.add))
-    step("va", V.tensor_scalar(T.rmask[:, :], T.ioB[:, :], 0, None, AluOpType.is_gt))
+    def quantise_w(a, b):
+        V.wait_ge(S["lw%d" % a], 16)
+        V.quantize_mx(T.wq[:, 128 * a:128 * b], T.ws[:, 128 * a:128 * b], T.wb[:, 512 * a:512 * b]).then_inc(S["qw%d" % a], 1)
 
+    V.memset(T.row[:, :], 0).then_inc(S.mz, 1)
     V.wait_ge(S.lsl, 32)
     for k in range(4):
         V.tensor_copy(T.o1[Q4 * k:Q4 * k + Q4, :], T.rsl[0:32, 0:H]).then_inc(S.o1r, 1)
@@ -212,136 +211,159 @@ def rank_program(g, core, T, topo):
     pick_sends("q", 1)
 
     def gather(k):
-        V.wait_ge(S["bc%d" % k], 1)
         need("va")
-        step("va", V.tensor_tensor(T["m%d" % k][:, :], T["prow%d" % k][:, 0:C].indirect(T.ox[:, H * k:H * k + H]),
-                                   T.dmask[:, :], AluOpType.mult))
+        step("va", V.tensor_copy(T["m%d" % k][:, :], T.row[:, :].indirect(T.ox[:, H * k:H * k + H])))
 
-    def scan(k):
+    def turn(k):
         need("va")
-        step("va", V.tensor_tensor_scan(T["z%d" % k][:, :], T.rmask[:, :], T["m%d" % k][:, :], 0.0, AluOpType.mult, AluOpType.add))
-
-    def ends(k):
-        return T["z%d" % k][:, 15:C:16]
+        step("va", V.transpose(T["z%d" % k][:, :], T["m%d" % k][:, :]))
 
     def fresh1(k):
         need("va")
-        step("va", V.tensor_scalar(T["cu%d" % k][:, :], ends(k), -1000.0, None, AluOpType.mult))
+        step("va", V.tensor_tensor(T["cu%d" % k][:, :], T["z%d" % k][:, 0:C:16], T.tn[:, H * k:H * k + H], AluOpType.mult))
 
     def fresh2(k):
         need("va")
-        step("va", V.tensor_tensor(T["cv%d" % k][:, :], T["cu%d" % k][:, :], T.t384[:, H * k:H * k + H], AluOpType.min))
-
-    def fresh3(k):
-        need("va")
-        step("va", V.tensor_tensor(T["cw%d" % k][:, :], T["cv%d" % k][:, :], ends(k), AluOpType.max))
+        step("va", V.tensor_tensor(T["cw%d" % k][:, :], T["cu%d" % k][:, :], T["z%d" % k][:, 0:C:16], AluOpType.max))
 
     def offsets(k, out):
         need("va")
         for d, c, a in runs:
             V.tensor_copy(T[out][:, a:a + 2 * c], T["cw%d" % k][:, 2 * d:2 * d + 2 * c]).then_inc(S[out + "r"], 1)
 
+    V.wait_ge(S.lsh, 128)
+    step("va", V.tensor_scalar(T.xh[:, :], T.rsh[:, 0:2 * H:2], 4, None, AluOpType.arith_shift_right))
+    for k in range(2):
+        step("va", V.tensor_scalar(T.xa[:, H // 2 * k:H // 2 * (k + 1)], T.rsh[:, H * k:H * k + H:2], 2 * H, H * k, AluOpType.mult, AluOpType.add))
     V.wait_ge(S.ls2, 96)
-    step("va", V.tensor_scalar(T.xh[:, :], T.rsl[:, H:3 * H], 4, None, AluOpType.arith_shift_right))
-    step("va", V.tensor_scalar(T.xa[:, :], T.rsl[:, H:3 * H], 0, H, AluOpType.max, AluOpType.mult))
+    step("vb", V.tensor_scalar(T.tp[:, :], T.rsl[:, H:3 * H], 0, NEW, AluOpType.max, AluOpType.add))
+    need("va")
+    step("va", V.tensor_scalar(T.xd[:, :], T.xh[:, :], 1 - 32 * H, None, AluOpType.mult))
     quantise("win0", 0, 0, "nw0")
     need("va")
-    step("va", V.tensor_scalar(T.xd[:, :], T.xh[:, :], 1 - 16 * H, None, AluOpType.mult))
-    step("vb", V.tensor_scalar(T.t384[:, :], T.rsl[:, H:3 * H], 0, NEW, AluOpType.max, AluOpType.add))
-    need("va")
     step("va", V.tensor_tensor(T.xc[:, :], T.xa[:, :], T.xd[:, :], AluOpType.add))
+    need("vb")
+    step("vb", V.tensor_scalar(T.tn[:, :], T.tp[:, :], -1, None, AluOpType.mult))
     need("va")
-    step("va", V.tensor_copy(T.ox[:, :], T.xc[:, :]))
+    step("va", V.tensor_copy(T.ox[:, 0:2 * H:2], T.xc[:, :]))
+    step("va", V.tensor_copy(T.ox[:, 1:2 * H:2], T.xc[:, :]))
+    V.wait_ge(S.mz, 1)
+    V.wait_ge(S.lrow, 128)
     gather(0)
     V.wait_ge(S.lx1, 16)
     quantise("win0", NEW, 1, "nw0")
-    scan(0)
+    turn(0)
     need("vb")
     fresh1(0)
     fresh2(0)
-    fresh3(0)
     offsets(0, "o2")
 
     V.wait_ge(S.nw0, 2)
     V.wait_ge(S.o2r, len(runs))
-    V.wait_ge(S.arq1, arrive[0])
+    V.wait_ge(S.arq1, arrive(1, "q", off + on))
     pick_sends("q", 2)
-    V.wait_ge(S.lpa, 128)
-    step("vb", V.tensor_scalar(T.pu[:, :], T.rpa[:, :], -1000, None, AluOpType.mult))
+    V.wait_ge(S.iot, 2)
+    step("vb", V.tensor_scalar(T.jl[:, :], T.ioJ[:, :], 15, None, AluOpType.bitwise_and))
     gather(1)
     need("vb")
-    step("vb", V.tensor_tensor(T.pm[:, :], T.pu[:, :], T.jt[:, :], AluOpType.min))
-    scan(1)
+    step("vb", V.tensor_tensor(T.jt[:, :], T.ioK[:, :], T.jl[:, :], AluOpType.subtract))
+    turn(1)
+    V.wait_ge(S.lpa, 128)
     need("vb")
-    step("vb", V.tensor_tensor(T.pr[:, :], T.pm[:, :], T.rpa[:, :], AluOpType.max))
+    step("vb", V.tensor_tensor(T.pu[:, :], T.rpa[:, :], T.jt[:, :], AluOpType.mult))
     fresh1(1)
     need("vb")
-    V.tensor_copy(T.po[:, :], T.pr[:, :]).then_inc(S.por, 1)
+    step("vb", V.tensor_tensor(T.pr[:, :], T.pu[:, :], T.rpa[:, :], AluOpType.max))
     fresh2(1)
+    need("vb")
+    V.tensor_copy(T.po[:, :], T.pr[:, :]).then_inc(S.por, 1)
+    offsets(1, "o3")
     V.wait_ge(S.por, 1)
     pick_cache("q", 1)
-    fresh3(1)
     V.wait_ge(S.lx2, 16)
     quantise("win1", NEW, 2, "nw1")
-    offsets(1, "o3")
 
     V.wait_ge(S.kq1, 1)
     V.wait_ge(S.nw1, 1)
     V.wait_ge(S.o3r, len(runs))
-    V.wait_ge(S.arq2, arrive[0])
+    V.wait_ge(S.arq2, arrive(2, "q", off + on))
     pick_sends("q", 3)
     pick_cache("q", 2)
-    V.wait_ge(S.lw, 16)
-    V.quantize_mx(T.wq[:, :], T.ws[:, :], T.wb[:, :]).then_inc(S.qw, 1)
+    fill_own("q")
+    quantise_w(0, 2)
+    quantise_w(2, 4)
     V.wait_ge(S.lx3, 16)
     quantise("win2", NEW, 3, "nw2")
 
-    V.wait_ge(S.kq2, 1)
-    V.wait_ge(S.nw2, 1)
-    V.wait_ge(S.arq3, arrive[0])
-    pick_cache("q", 3)
-    V.wait_ge(S.mm4, 1)
-    V.tensor_copy(T.yb[:, 3 * C + CUT:4 * C], T.ps[:, 4 * 512 + 2 * CUT - C:4 * 512 + CUT]).then_inc(S.yc4, 1)
+    home = sorted(on + [r])
+    regions = {4: (NEW, NEW, C), 5: None, 6: None}
+    for bank, ranks in ((5, home), (6, off)):
+        a = C + CAPP * ranks[0]
+        w = CAPP * len(ranks)
+        regions[bank] = (a - (MIN - w) if a == C else a, a, w)
+
+    for bank in (4, 5, 6):
+        s, a, w = regions[bank]
+        V.wait_ge(S["mm%d" % bank], 1)
+        V.tensor_copy(T.yw[:, a:a + w], T.ps[:, BANK * bank + a - s:BANK * bank + a - s + w]).then_inc(S.ywr, 1)
+    V.wait_ge(S.ywr, 4)
+    h = H * (R - 1)
+    V.tensor_copy(T.yb[:, R * C:R * C + C // 2], T.yw[:, :].indirect(T.po[:, h:h + H // 2])).then_inc(S.yc3, 1)
 
     A.wait_ge(S.o1r, 4)
     A.wait_ge(S.q0, 1)
     pick_sends("s", 1)
     A.wait_ge(S.nw0, 2)
     A.wait_ge(S.o2r, len(runs))
-    A.wait_ge(S.ars1, arrive[1])
+    A.wait_ge(S.ars1, arrive(1, "s", off + on))
     pick_sends("s", 2)
     A.wait_ge(S.por, 1)
     pick_cache("s", 1)
     A.wait_ge(S.ks1, 1)
     A.wait_ge(S.nw1, 1)
     A.wait_ge(S.o3r, len(runs))
-    A.wait_ge(S.ars2, arrive[1])
+    A.wait_ge(S.ars2, arrive(2, "s", off + on))
     pick_sends("s", 3)
     pick_cache("s", 2)
+    fill_own("s")
     for t in range(R):
         A.wait_ge(S["mm%d" % t], 1)
-        A.activation(T.yb[:, C * t:C * t + C], T.ps[:, 512 * t:512 * t + C], ActivationFunctionType.Copy).then_inc(S["yc%d" % t], 1)
-    A.wait_ge(S.ks2, 1)
-    A.wait_ge(S.nw2, 1)
-    A.wait_ge(S.ars3, arrive[1])
-    pick_cache("s", 3)
+        A.activation(T.yb[:, C * t:C * t + C], T.ps[:, BANK * t:BANK * t + C], ActivationFunctionType.Copy).then_inc(S["yc%d" % t], 1)
     A.wait_ge(S.mm3, 1)
-    A.activation(T.yb[:, 3 * C:3 * C + CUT], T.ps[:, 3 * 512:3 * 512 + CUT], ActivationFunctionType.Copy).then_inc(S.yc3, 1)
+    A.activation(T.yw[:, 0:C], T.ps[:, BANK * 3:BANK * 3 + C], ActivationFunctionType.Copy).then_inc(S.ywr, 1)
+    A.wait_ge(S.ywr, 4)
+    A.activation(T.yb[:, R * C + C // 2:R * C + C], T.yw[:, :].indirect(T.po[:, h + H // 2:h + H]), ActivationFunctionType.Copy).then_inc(S.yc3, 1)
 
-    def product(k, b, a, w):
-        t = min(k, R)
-        g.tensor.matmul_mx(T.ps[:, 512 * k:512 * k + w], T.wq[:, 128 * t:128 * t + 128], T.ws[:, 128 * t:128 * t + 128],
-                           T[b + "q"][:, a:a + w], T[b + "s"][:, a:a + w], True, True).then_inc(S["mm%d" % k], 1)
+    P = g.tensor
 
-    g.tensor.wait_ge(S.qw, 1)
-    g.tensor.wait_ge(S.q0, 1)
+    def product(bank, b, a, w):
+        t = min(bank, R)
+        P.matmul_mx(T.ps[:, BANK * bank:BANK * bank + w], T.wq[:, 128 * t:128 * t + 128], T.ws[:, 128 * t:128 * t + 128],
+                    T[b + "q"][:, a:a + w], T[b + "s"][:, a:a + w], True, True).then_inc(S["mm%d" % bank], 1)
+
+    P.wait_ge(S.q0, 1)
+    P.wait_ge(S.qw0, 1)
     product(0, "k0", 0, C)
-    for k, b, a, w in ((1, "win1", 0, C), (2, "win2", 0, C), (3, "k3", 0, CUT), (4, "k3", C - CUT, CUT)):
-        g.tensor.wait_ge(S["kq%d" % k], 1)
-        g.tensor.wait_ge(S["ks%d" % k], 1)
-        product(k, b, a, w)
+    P.wait_ge(S.kq1, 1)
+    P.wait_ge(S.ks1, 1)
+    product(1, "win1", 0, C)
+    P.wait_ge(S.qw2, 1)
+    P.wait_ge(S.kq2, 1)
+    P.wait_ge(S.ks2, 1)
+    product(2, "win2", 0, C)
+    product(3, "win2", 0, C)
+    P.wait_ge(S.nw2, 1)
+    product(4, "win2", NEW, C)
+    P.wait_ge(S.kfq, 1)
+    P.wait_ge(S.kfs, 1)
+    P.wait_ge(S.anq, arrive(R, "q", on))
+    P.wait_ge(S.ans, arrive(R, "s", on))
+    product(5, "win2", regions[5][0], MIN)
+    P.wait_ge(S.arq3, arrive(R, "q", off))
+    P.wait_ge(S.ars3, arrive(R, "s", off))
+    product(6, "win2", regions[6][0], MIN)
 
-    for k, (a, b) in enumerate(((0, C), (C, 2 * C), (2 * C, 3 * C), (3 * C, 3 * C + CUT), (3 * C + CUT, 4 * C))):
-        Y.wait_ge(S["yc%d" % k], 1)
-        Y.dma_start(T.y[:, a:b], T.yb[:, a:b]).then_inc(S.st, 16)
-    Y.wait_ge(S.st, 16 * (R + 2))
+    for t in range(R + 1):
+        Y.wait_ge(S["yc%d" % t], 2 if t == R else 1)
+        Y.dma_start(T.y[:, C * t:C * t + C], T.yb[:, C * t:C * t + C]).then_inc(S.st, 16)
+    Y.wait_ge(S.st, 16 * (R + 1))

from concourse.bass import DstId, RemoteDMATransfer
from concourse.mybir import dt, AluOpType, ActivationFunctionType

C, R, CAPP, N = 192, 3, 32, 6
WIN = 3 * C
NEW = 2 * C
H = C // 16
Q4 = 128 // 4
MIN = 128
BANK = 512
PARTS = ("a", "b")
CALLS = {1: (("q", "a"), ("s", "a"), ("q", "b"), ("s", "b"))}
CALLS[2] = CALLS[3] = (("q", "a"), ("q", "b"), ("s", "a"), ("s", "b"))

CODE, PLANE = "float8_e4m3fn_x4", "uint8"
SCRATCH = {
    "xb": ("sbuf", [128, 4 * C * (R + 1)], "bfloat16"),
    "wb": ("sbuf", [128, 512 * (R + 1)], "bfloat16"),
    "wq": ("sbuf", [128, 128 * (R + 1)], CODE), "ws": ("sbuf", [128, 128 * (R + 1)], PLANE),
    "k0q": ("sbuf", [128, C], CODE), "k0s": ("sbuf", [128, C], PLANE),
    "yb": ("sbuf", [128, C * (R + 1)], "float32"), "yw": ("sbuf", [128, WIN], "float32"),
    "ps": ("psum", [128, BANK * 7], "float32"),
    "rsl": ("sbuf", [128, 3 * H], "int32"), "rpa": ("sbuf", [128, 3 * H], "int32"),
    "rsh": ("sbuf", [128, 2 * H], "int32"), "row": ("sbuf", [128, 2 * C], "int32"),
    "xh": ("sbuf", [128, H], "int32"), "xa": ("sbuf", [128, H], "int32"),
    "xd": ("sbuf", [128, H], "int32"), "xc": ("sbuf", [128, H], "int32"), "ox": ("sbuf", [128, 2 * H], "uint16"),
    "tp": ("sbuf", [128, 2 * H], "float32"), "tn": ("sbuf", [128, 2 * H], "float32"),
    "ioJ": ("sbuf", [128, 3 * H], "int32"), "ioK": ("sbuf", [128, 3 * H], "int32"),
    "jl": ("sbuf", [128, 3 * H], "int32"), "jt": ("sbuf", [128, 3 * H], "int32"),
    "pu": ("sbuf", [128, 3 * H], "int32"), "pr": ("sbuf", [128, 3 * H], "int32"),
    "o1": ("sbuf", [128, H], "uint16"), "o2": ("sbuf", [128, H], "uint16"), "o3": ("sbuf", [128, H], "uint16"),
    "po": ("sbuf", [128, 3 * H], "uint16"),
}
for _k in range(2):
    SCRATCH["m%d" % _k] = ("sbuf", [128, C], "float32")
    SCRATCH["z%d" % _k] = ("sbuf", [128, C], "float32")
    for _n in ("u", "w"):
        SCRATCH["c%s%d" % (_n, _k)] = ("sbuf", [128, H], "float32")
for _t in range(R):
    SCRATCH["win%dq" % _t] = ("sbuf", [128, WIN], CODE)
    SCRATCH["win%ds" % _t] = ("sbuf", [128, WIN], PLANE)
    SCRATCH["sn%dq" % (_t + 1)] = ("sbuf", [128, C], CODE)
    SCRATCH["sn%ds" % (_t + 1)] = ("sbuf", [128, C], PLANE)

SEMAPHORES = (["lx0", "lx1", "lx2", "lx3", "lw0", "lw2", "lsl", "ls2", "lsh", "lpa", "lrow", "st", "mz", "iot",
               "va", "vb", "o1r", "o2r", "o3r", "por", "q0", "nw0", "nw1", "nw2", "qw0", "qw2", "lq1", "lq2", "left",
               "kfq", "kfs", "anq", "ans", "ywr"]
              + ["%s%d" % (n, t) for t in (1, 2, 3) for n in ("kq", "ks", "arq", "ars")]
              + ["p%s%d%s" % (n, t, w) for t in (1, 2, 3) for n in "qs" for w in PARTS]
              + ["mm%d" % t for t in range(7)] + ["yc%d" % t for t in range(4)])


def peers(topo, cores, r):
    ds = [d for d in range(len(cores)) if d != r]
    home = topo.chip(cores[r])
    return [d for d in ds if topo.chip(cores[d]) != home], [d for d in ds if topo.chip(cores[d]) == home]


def bits(es):
    return sum(1 << e for e in es)


def parts_of(topo, cores, r, t):
    off, on = peers(topo, cores, r)
    return {"a": off, "b": on} if t == 1 else {"a": off[:2], "b": off[2:] + on}


def engines_of(topo, cores, r, t):
    off, on = peers(topo, cores, r)
    far = topo.engines(cores[r], cores[off[0]])
    near = [e for e in topo.engines(cores[r], cores[on[0]]) if e not in far]
    h, q = len(far) // 2, len(far) // 4
    a, b = far[:h], far[h:]
    if t == 1:
        plan = {off[0]: (a, b), off[1]: (b[:q], a[:q]), off[2]: (b[q:], a[q:])}
    else:
        plan = {off[0]: (a, a), off[1]: (b, b), off[2]: (far, far)}
    k = len(near) // 2
    for i, d in enumerate(on):
        plan[d] = (near[i * k:i * k + k], near[i * k:i * k + k])
    return plan


def rank_program(g, core, T, topo):
    r = T.rank_of(core)
    if r is None:
        return
    S, V, A, Y = T.sem, g.vector, g.scalar, g.sync
    cores = list(T.cores)
    rounds = range(1, R + 1)
    off, on = peers(topo, cores, r)
    plan = {t: engines_of(topo, cores, r, t) for t in rounds}
    to = {t: parts_of(topo, cores, r, t) for t in rounds}

    def arrive(t, part, sources):
        return sum(len(engines_of(topo, cores, q, t)[r]["qs".index(part)]) for q in sources)

    order = to[2]["a"] + to[2]["b"]
    at = {1: {d: CAPP * d for d in range(N)}}
    at[2] = at[3] = {d: CAPP * i for i, d in enumerate(order)}
    runs = []
    for d in order:
        if runs and runs[-1][0] + runs[-1][1] == d:
            runs[-1][1] += 1
        else:
            runs.append([d, 1, at[2][d] // 16])

    XP = 4 * C

    def load_x(t):
        Y.dma_start(T.xb[:, XP * t:XP * t + XP], T.x[:, XP * t:XP * t + XP]).then_inc(S["lx%d" % t], 16)

    def load_w(a, b):
        Y.dma_start(T.wb[:, 512 * a:512 * b], T.w[:, 512 * a:512 * b]).then_inc(S["lw%d" % a], 16)

    def group(queue, buf, src, k, sem):
        queue.dma_start(T[buf][16 * k:16 * k + 16, :], src[:, :]).then_inc(S[sem], 16)

    def behind(t):
        Y.wait_ge(S["lq%d" % t], sum(len(plan[t][d][0]) for d in to[t]["a"]))

    load_x(0)
    group(A, "rsl", T.sl, 0, "lsl")
    group(A, "rsl", T.sl, 1, "lsl")
    for k in range(8):
        o = k % 2
        A.dma_start(T.rsh[16 * k:16 * k + 16, 0:2 * H - o], T.sl[:, H + o:3 * H]).then_inc(S.lsh, 16)
    Y.wait_ge(S.mz, 1)
    for k in range(8):
        Y.dma_start(T.row[16 * k:16 * k + 1, :], T.pa[:, 0:2 * H]).then_inc(S.lrow, 16)
    for k in range(2, 8):
        group(Y, "rsl", T.sl, k, "ls2")
    load_x(1)
    load_w(0, 2)
    for k in range(8):
        group(Y, "rpa", T.pa, k, "lpa")
    load_x(2)
    behind(1)
    load_w(2, 4)
    behind(2)
    load_x(3)

    g.iota(T.ioJ[:, :], [[0, 3 * H]], 0, 1).then_inc(S.iot, 1)
    g.iota(T.ioK[:, :], [[0, R], [-16, H]], -NEW, 0).then_inc(S.iot, 1)

    waits = 0
    for t in rounds:
        for part, where in CALLS[t]:
            src, dst, i = T["sn%d%s" % (t, part)], T["win%d%s" % (t - 1, part)], "qs".index(part)
            trs, n = [], 0
            for d in to[t][where]:
                rid, pid = topo.addr(cores[d])[:2]
                a, b = at[t][d], C + CAPP * r
                sv, dv = src[:, a:a + CAPP], dst[:, b:b + CAPP]
                if part == "q":
                    sv, dv = sv.bitcast(dt.uint8), dv.bitcast(dt.uint8)
                sem = "an" + part if t == R and d in on else "ar%s%d" % (part, t)
                trs.append(RemoteDMATransfer(dst_ids=[DstId(rid=rid, pnc=pid)], dma_engine_mask=bits(plan[t][d][i]),
                                             remote_sem=S[sem], srcs=[sv], dsts=[dv]))
                n += len(plan[t][d][i])
            first = t < R and (part, where) == CALLS[t][0]
            waits += 0 if first else n
            g.wait_ge(S["p%s%d%s" % (part, t, where)], 1)
            g.remote_dma_fused(trs, local_sem=S["lq%d" % t] if first else S.left)
    g.wait_ge(S.left, waits)

    n = {"va": 0, "vb": 0}

    def step(chain, call):
        call.then_inc(S[chain], 1)
        n[chain] += 1

    def need(chain):
        V.wait_ge(S[chain], n[chain])

    def pick(part, out, o, win, n_win, offs, w, sem):
        if part == "q":
            V.tensor_copy(T[out + "q"][:, o:o + w].bitcast(dt.uint32),
                          T[win + "q"][:, 0:n_win].bitcast(dt.uint32).indirect(offs)).then_inc(S[sem], 1)
        else:
            A.activation(T[out + "s"][:, o:o + w], T[win + "s"][:, 0:n_win].indirect(offs), ActivationFunctionType.Copy).then_inc(S[sem], 1)

    def pick_sends(part, t):
        for w in PARTS:
            a, b = min(at[t][d] for d in to[t][w]), max(at[t][d] for d in to[t][w]) + CAPP
            pick(part, "sn%d" % t, a, "k0" if t == 1 else "win%d" % (t - 2), C if t == 1 else WIN,
                 T["o%d" % t][:, a // 16:b // 16], b - a, "p%s%d%s" % (part, t, w))

    def pick_cache(part, t):
        pick(part, "win%d" % t, 0, "win%d" % (t - 1), WIN, T.po[:, H * (t - 1):H * t], C, "k%s%d" % (part, t))

    def fill_own(part):
        t = R - 1
        pick(part, "win%d" % t, C + CAPP * r, "win%d" % (t - 1), WIN, T.po[:, H * (t - 1):H * (t - 1) + CAPP // 16], CAPP, "kf" + part)

    def quantise(b, a, t, sem):
        V.quantize_mx(T[b + "q"][:, a:a + C], T[b + "s"][:, a:a + C], T.xb[:, XP * t:XP * t + XP]).then_inc(S[sem], 1)

    def quantise_w(a, b):
        V.wait_ge(S["lw%d" % a], 16)
        V.quantize_mx(T.wq[:, 128 * a:128 * b], T.ws[:, 128 * a:128 * b], T.wb[:, 512 * a:512 * b]).then_inc(S["qw%d" % a], 1)

    V.memset(T.row[:, :], 0).then_inc(S.mz, 1)
    V.wait_ge(S.lsl, 32)
    for k in range(4):
        V.tensor_copy(T.o1[Q4 * k:Q4 * k + Q4, :], T.rsl[0:32, 0:H]).then_inc(S.o1r, 1)
    V.wait_ge(S.lx0, 16)
    quantise("k0", 0, 0, "q0")
    V.wait_ge(S.o1r, 4)
    V.wait_ge(S.q0, 1)
    pick_sends("q", 1)

    def gather(k):
        need("va")
        step("va", V.tensor_copy(T["m%d" % k][:, :], T.row[:, :].indirect(T.ox[:, H * k:H * k + H])))

    def turn(k):
        need("va")
        step("va", V.transpose(T["z%d" % k][:, :], T["m%d" % k][:, :]))

    def fresh1(k):
        need("va")
        step("va", V.tensor_tensor(T["cu%d" % k][:, :], T["z%d" % k][:, 0:C:16], T.tn[:, H * k:H * k + H], AluOpType.mult))

    def fresh2(k):
        need("va")
        step("va", V.tensor_tensor(T["cw%d" % k][:, :], T["cu%d" % k][:, :], T["z%d" % k][:, 0:C:16], AluOpType.max))

    def offsets(k, out):
        need("va")
        for d, c, a in runs:
            V.tensor_copy(T[out][:, a:a + 2 * c], T["cw%d" % k][:, 2 * d:2 * d + 2 * c]).then_inc(S[out + "r"], 1)

    V.wait_ge(S.lsh, 128)
    step("va", V.tensor_scalar(T.xh[:, :], T.rsh[:, 0:2 * H:2], 4, None, AluOpType.arith_shift_right))
    for k in range(2):
        step("va", V.tensor_scalar(T.xa[:, H // 2 * k:H // 2 * (k + 1)], T.rsh[:, H * k:H * k + H:2], 2 * H, H * k, AluOpType.mult, AluOpType.add))
    V.wait_ge(S.ls2, 96)
    step("vb", V.tensor_scalar(T.tp[:, :], T.rsl[:, H:3 * H], 0, NEW, AluOpType.max, AluOpType.add))
    need("va")
    step("va", V.tensor_scalar(T.xd[:, :], T.xh[:, :], 1 - 32 * H, None, AluOpType.mult))
    quantise("win0", 0, 0, "nw0")
    need("va")
    step("va", V.tensor_tensor(T.xc[:, :], T.xa[:, :], T.xd[:, :], AluOpType.add))
    need("vb")
    step("vb", V.tensor_scalar(T.tn[:, :], T.tp[:, :], -1, None, AluOpType.mult))
    need("va")
    step("va", V.tensor_copy(T.ox[:, 0:2 * H:2], T.xc[:, :]))
    step("va", V.tensor_copy(T.ox[:, 1:2 * H:2], T.xc[:, :]))
    V.wait_ge(S.mz, 1)
    V.wait_ge(S.lrow, 128)
    gather(0)
    V.wait_ge(S.lx1, 16)
    quantise("win0", NEW, 1, "nw0")
    turn(0)
    need("vb")
    fresh1(0)
    fresh2(0)
    offsets(0, "o2")

    V.wait_ge(S.nw0, 2)
    V.wait_ge(S.o2r, len(runs))
    V.wait_ge(S.arq1, arrive(1, "q", off + on))
    pick_sends("q", 2)
    V.wait_ge(S.iot, 2)
    step("vb", V.tensor_scalar(T.jl[:, :], T.ioJ[:, :], 15, None, AluOpType.bitwise_and))
    gather(1)
    need("vb")
    step("vb", V.tensor_tensor(T.jt[:, :], T.ioK[:, :], T.jl[:, :], AluOpType.subtract))
    turn(1)
    V.wait_ge(S.lpa, 128)
    need("vb")
    step("vb", V.tensor_tensor(T.pu[:, :], T.rpa[:, :], T.jt[:, :], AluOpType.mult))
    fresh1(1)
    need("vb")
    step("vb", V.tensor_tensor(T.pr[:, :], T.pu[:, :], T.rpa[:, :], AluOpType.max))
    fresh2(1)
    need("vb")
    V.tensor_copy(T.po[:, :], T.pr[:, :]).then_inc(S.por, 1)
    offsets(1, "o3")
    V.wait_ge(S.por, 1)
    pick_cache("q", 1)
    V.wait_ge(S.lx2, 16)
    quantise("win1", NEW, 2, "nw1")

    V.wait_ge(S.kq1, 1)
    V.wait_ge(S.nw1, 1)
    V.wait_ge(S.o3r, len(runs))
    V.wait_ge(S.arq2, arrive(2, "q", off + on))
    pick_sends("q", 3)
    pick_cache("q", 2)
    fill_own("q")
    quantise_w(0, 2)
    quantise_w(2, 4)
    V.wait_ge(S.lx3, 16)
    quantise("win2", NEW, 3, "nw2")

    home = sorted(on + [r])
    regions = {4: (NEW, NEW, C), 5: None, 6: None}
    for bank, ranks in ((5, home), (6, off)):
        a = C + CAPP * ranks[0]
        w = CAPP * len(ranks)
        regions[bank] = (a - (MIN - w) if a == C else a, a, w)

    for bank in (4, 5, 6):
        s, a, w = regions[bank]
        V.wait_ge(S["mm%d" % bank], 1)
        V.tensor_copy(T.yw[:, a:a + w], T.ps[:, BANK * bank + a - s:BANK * bank + a - s + w]).then_inc(S.ywr, 1)
    V.wait_ge(S.ywr, 4)
    h = H * (R - 1)
    V.tensor_copy(T.yb[:, R * C:R * C + C // 2], T.yw[:, :].indirect(T.po[:, h:h + H // 2])).then_inc(S.yc3, 1)

    A.wait_ge(S.o1r, 4)
    A.wait_ge(S.q0, 1)
    pick_sends("s", 1)
    A.wait_ge(S.nw0, 2)
    A.wait_ge(S.o2r, len(runs))
    A.wait_ge(S.ars1, arrive(1, "s", off + on))
    pick_sends("s", 2)
    A.wait_ge(S.por, 1)
    pick_cache("s", 1)
    A.wait_ge(S.ks1, 1)
    A.wait_ge(S.nw1, 1)
    A.wait_ge(S.o3r, len(runs))
    A.wait_ge(S.ars2, arrive(2, "s", off + on))
    pick_sends("s", 3)
    pick_cache("s", 2)
    fill_own("s")
    for t in range(R):
        A.wait_ge(S["mm%d" % t], 1)
        A.activation(T.yb[:, C * t:C * t + C], T.ps[:, BANK * t:BANK * t + C], ActivationFunctionType.Copy).then_inc(S["yc%d" % t], 1)
    A.wait_ge(S.mm3, 1)
    A.activation(T.yw[:, 0:C], T.ps[:, BANK * 3:BANK * 3 + C], ActivationFunctionType.Copy).then_inc(S.ywr, 1)
    A.wait_ge(S.ywr, 4)
    A.activation(T.yb[:, R * C + C // 2:R * C + C], T.yw[:, :].indirect(T.po[:, h + H // 2:h + H]), ActivationFunctionType.Copy).then_inc(S.yc3, 1)

    P = g.tensor

    def product(bank, b, a, w):
        t = min(bank, R)
        P.matmul_mx(T.ps[:, BANK * bank:BANK * bank + w], T.wq[:, 128 * t:128 * t + 128], T.ws[:, 128 * t:128 * t + 128],
                    T[b + "q"][:, a:a + w], T[b + "s"][:, a:a + w], True, True).then_inc(S["mm%d" % bank], 1)

    P.wait_ge(S.q0, 1)
    P.wait_ge(S.qw0, 1)
    product(0, "k0", 0, C)
    P.wait_ge(S.kq1, 1)
    P.wait_ge(S.ks1, 1)
    product(1, "win1", 0, C)
    P.wait_ge(S.qw2, 1)
    P.wait_ge(S.kq2, 1)
    P.wait_ge(S.ks2, 1)
    product(2, "win2", 0, C)
    product(3, "win2", 0, C)
    P.wait_ge(S.nw2, 1)
    product(4, "win2", NEW, C)
    P.wait_ge(S.kfq, 1)
    P.wait_ge(S.kfs, 1)
    P.wait_ge(S.anq, arrive(R, "q", on))
    P.wait_ge(S.ans, arrive(R, "s", on))
    product(5, "win2", regions[5][0], MIN)
    P.wait_ge(S.arq3, arrive(R, "q", off))
    P.wait_ge(S.ars3, arrive(R, "s", off))
    product(6, "win2", regions[6][0], MIN)

    for t in range(R + 1):
        Y.wait_ge(S["yc%d" % t], 2 if t == R else 1)
        Y.dma_start(T.y[:, C * t:C * t + C], T.yb[:, C * t:C * t + C]).then_inc(S.st, 16)
    Y.wait_ge(S.st, 16 * (R + 1))
